import numpy as np
import ml_dtypes


def mxq(x, axis, fmt="e4m3"):
    dtype, down = {"e4m3": (ml_dtypes.float8_e4m3fn, 7), "e5m2": (ml_dtypes.float8_e5m2, 14)}[fmt]
    v = np.moveaxis(np.asarray(x, np.float32).astype(ml_dtypes.bfloat16).astype(np.float64), axis, -1)
    blocks = v.reshape(v.shape[:-1] + (-1, 32))
    amax = np.abs(blocks).max(-1, keepdims=True)
    byte = np.maximum(np.where(amax > 0, np.frexp(amax)[1] - 1 + 127, 0) - down, 1)
    scale = np.exp2(byte - 127.0)
    codes = (blocks / scale).astype(np.float32).astype(dtype).astype(np.float64)
    return np.moveaxis((codes * scale).reshape(v.shape), -1, axis)


WIDE = False


def mx_kscale(k):
    if not WIDE:
        return np.ones(k)
    levels = np.array([10, -10, 5, -5, 0])
    if k % 512:
        return np.exp2(np.random.permutation(np.resize(levels, k // 32))).repeat(32)
    a = np.empty((k // 512, 16))
    for p in range(k // 512):
        a[p, :8] = np.random.permutation(np.resize(levels, 8))
        for g in range(8):
            far = levels[np.abs(levels - a[p, g]) >= 10]
            a[p, g + 8] = far[np.random.randint(len(far))]
    return np.exp2(a.ravel()).repeat(32)


def f64(x):
    return np.asarray(x).astype(np.float64)


def striped(idx):
    return np.tile(idx.reshape(-1, 16).T, (8, 1)).astype(np.uint16)


def unstriped(offs):
    return offs[:16].T.reshape(-1).astype(np.int64)


E2M1 = np.array([0.0, 0.5, 1.0, 1.5, 2.0, 3.0, 4.0, 6.0, -0.0, -0.5, -1.0, -1.5, -2.0, -3.0, -4.0, -6.0])


def pack_weight(w, fmt):
    k, n = w.shape
    w = f64(np.asarray(w, np.float32).astype(ml_dtypes.bfloat16)).reshape(k // 32, 32, n)
    amax = np.abs(w).max(1)
    if fmt == "e4m3":
        byte = np.frexp(amax)[1] - 1 + 127 - 7
    else:
        mant, ex = np.frexp(amax / 6.0)
        byte = np.where(mant > 0.5, ex, ex - 1) + 127
    byte = np.clip(np.where(amax > 0, byte, 1), 1, 254)
    scaled = (w * np.exp2(127.0 - byte)[:, None, :]).reshape(k, n).astype(np.float32)
    by_word = np.ascontiguousarray(scaled.reshape(k // 512, 128, 4, n).transpose(0, 1, 3, 2))
    if fmt == "e4m3":
        words = by_word.astype(ml_dtypes.float8_e4m3fn).view(np.uint8)
    else:
        c = by_word.astype(ml_dtypes.float4_e2m1fn).view(np.uint8) & 0xF
        words = (c[..., 0::2] | (c[..., 1::2] << 4)).reshape(k // 512, 128, 2 * n)
    return np.ascontiguousarray(words), np.ascontiguousarray(byte.astype(np.uint8).reshape(k // 512, 16, n))


def unpack_weight(words, scales, fmt):
    g, _, n = scales.shape
    words = np.ascontiguousarray(words).reshape(g, 128, n, -1)
    if fmt == "e4m3":
        vals = words.view(ml_dtypes.float8_e4m3fn).astype(np.float64)
    else:
        nib = np.empty((g, 128, n, 4), np.uint8)
        nib[..., 0::2] = words & 0xF
        nib[..., 1::2] = words >> 4
        vals = E2M1[nib]
    vals = vals * np.repeat(np.exp2(scales.astype(np.float64) - 127.0), 8, axis=1)[..., None]
    return vals.transpose(0, 1, 3, 2).reshape(g * 512, n)


def gelu(v):
    return 0.5 * v * (1.0 + np.tanh(np.sqrt(2.0 / np.pi) * (v + 0.044715 * v**3)))


K, H, T, S, T2, P = 1024, 512, 4096, 1024, 2048, 1024


def setup_inputs():
    n = np.random.standard_normal
    s = mx_kscale(K)[:, None]
    u = mx_kscale(H)[:, None]
    d = {}
    d["tab_words"], d["tab_scales"] = pack_weight(n((K, T)) * s, "e4m3")
    d["offs"] = striped(np.random.permutation(T)[:S])
    d["w1"] = (0.8 * n((K, H)) / s / K ** 0.5).astype(np.float32)
    d["w2_words"], d["w2_scales"] = pack_weight(0.8 * n((K, H)) / s / K ** 0.5, "e2m1")
    d["w3"] = (n((K, H)) / s * u.T / K ** 0.5).astype(np.float32)
    d["page0"] = (n((H, T2)) * u).astype(np.float32)
    d["wgs"] = np.exp(0.3 * n((128, S))).astype(np.float32)
    d["offs2"] = striped(np.random.permutation(T2)[:S])
    d["offs3"] = striped(np.random.permutation(T2)[:P])
    d["gain"] = np.exp(0.4 * n(H)).astype(np.float32)
    d["w4_words"], d["w4_scales"] = pack_weight(1.2 * n((H, H)) / u / H ** 0.5, "e4m3")
    d["res"] = (0.9 * np.exp(0.3 * n(H)) / u[:, 0]).astype(np.float32)
    d["page1"] = (0.7 * n((H, T2))).astype(np.float32)
    d["wgo"] = np.exp(0.3 * n((128, P))).astype(np.float32)
    d["offs4"] = striped(np.random.permutation(T2)[:P])
    return d


def reference(tab_words, tab_scales, offs, w1, w2_words, w2_scales, w3, page0, wgs, offs2, offs3, gain,
              w4_words, w4_scales, res, page1, wgo, offs4):
    v = unpack_weight(tab_words, tab_scales, "e4m3")[:, unstriped(offs)]
    a = mxq(f64(w1), 0, "e4m3").T @ v
    b = unpack_weight(w2_words, w2_scales, "e2m1").T @ v
    c = mxq(f64(w3), 0, "e4m3").T @ v
    h = np.abs(a - b) * c
    page = f64(page0).copy()
    page[:, unstriped(offs2)] = np.tile(f64(wgs), (H // 128, 1)) * h
    x = f64(gain)[:, None] * page[:, unstriped(offs3)]
    e = unpack_weight(w4_words, w4_scales, "e4m3").T @ mxq(x, 0, "e4m3")
    y = 1.0 / (1.0 + np.exp(-(e + f64(res)[:, None] * x)))
    out = f64(page1).copy()
    out[:, unstriped(offs4)] = np.tile(f64(wgo), (H // 128, 1)) * y
    return out

@@ -1,0 +1,277 @@
+from contextlib import ExitStack
+
+import concourse.mybir as mybir
+from concourse.masks import make_identity
+
+K, H, T, S, T2, NP = 1024, 512, 4096, 1024, 2048, 1024
+FLOPS = 2 * 3 * K * H * S + 2 * H * H * NP
+
+F32 = mybir.dt.float32
+BF16 = mybir.dt.bfloat16
+I32 = mybir.dt.int32
+U32 = mybir.dt.uint32
+U16 = mybir.dt.uint16
+U8 = mybir.dt.uint8
+FP8X4 = mybir.dt.float8_e4m3fn_x4
+FP4X4 = mybir.dt.float4_e2m1fn_x4
+ACT = mybir.ActivationFunctionType
+ALU = mybir.AluOpType
+
+P = 128
+PASSES = K // 512
+SLICES = H // P
+QUARTER = 256
+
+
+def tile_list_slab_vein_page_kernel(tc, tab_words, tab_scales, offs, w1, w2_words, w2_scales, w3, page0,
+                                             wgs, offs2, offs3, gain, w4_words, w4_scales, res, page1, wgo, offs4,
+                                             out):
+    nc = tc.nc
+    with ExitStack() as ctx:
+        keep = ctx.enter_context(tc.tile_pool(name="keep", bufs=1))
+        ring = ctx.enter_context(tc.tile_pool(name="ring", bufs=2))
+        psum = ctx.enter_context(tc.psum_pool(name="psum", bufs=2))
+
+        def entries(lst, lo, hi):
+            return lst[:, lo // 16 : hi // 16]
+
+        l1 = keep.tile([P, S // 16], U16, name="l1")
+        l2 = keep.tile([P, S // 16], U16, name="l2")
+        l3 = keep.tile([P, NP // 16], U16, name="l3")
+        l4 = keep.tile([P, NP // 16], U16, name="l4")
+        tw = [keep.tile([P, T], U32, name=f"tw{a}", align_bytes=64) for a in range(PASSES)]
+        ts = keep.tile([P, PASSES, T], U8, name="ts", align_bytes=64)
+        vw = [keep.tile([P, S], U32, name=f"vw{a}", align_bytes=64) for a in range(PASSES)]
+        vs = [keep.tile([P, S], U8, name=f"vs{a}", align_bytes=64) for a in range(PASSES)]
+        w2w = keep.tile([P, PASSES, 2 * H], U8, name="w2w", align_bytes=64)
+        w2s = keep.tile([P, PASSES, H], U8, name="w2s", align_bytes=64)
+        w4w = keep.tile([P, H], U32, name="w4w", align_bytes=64)
+        w4s = keep.tile([P, H], U8, name="w4s", align_bytes=64)
+        pg0 = [keep.tile([P, T2], F32, name=f"pg0_{s}") for s in range(SLICES)]
+        pg1 = [keep.tile([P, T2], F32, name=f"pg1_{s}") for s in range(SLICES)]
+        wgs_t = keep.tile([P, S], F32, name="wgs_t")
+        wgo_t = keep.tile([P, NP], F32, name="wgo_t")
+        gain_t = keep.tile([P, SLICES], F32, name="gain_t")
+        res_t = keep.tile([P, SLICES], F32, name="res_t")
+        rg_t = keep.tile([P, SLICES], F32, name="rg_t")
+        id16 = keep.tile([P, P], BF16, name="id16")
+        id32 = keep.tile([P, P], F32, name="id32")
+        groups = [(0, 1), (1, 2), (2, 4)]
+        raw = {}
+        for wi in range(2):
+            for lo, hi in groups:
+                for a in range(PASSES):
+                    raw[wi, lo, a] = keep.tile([P, 4, (hi - lo) * P], F32, name=f"raw{wi}_{lo}_{a}")
+        grp = {}
+        wq = {}
+        wsc = {}
+        for wi in range(2):
+            for s in range(SLICES):
+                grp[wi, s] = keep.tile([P, 512], F32, name=f"grp{wi}_{s}", align_bytes=64)
+                wq[wi, s] = keep.tile([P, PASSES * P], U32, name=f"wq{wi}_{s}", align_bytes=64)
+                wsc[wi, s] = keep.tile([P, PASSES * P], U8, name=f"wsc{wi}_{s}", align_bytes=64)
+        late = keep.tile([P, 3 * 512], F32, name="late")
+        xq = keep.tile([P, NP], U32, name="xq", align_bytes=64)
+        xs = keep.tile([P, NP], U8, name="xs", align_bytes=64)
+        xt = [keep.tile([P, 512], F32, name=f"xt{q}", align_bytes=64) for q in range(3)]
+        xt.append(xt[0])
+        xi = [keep.tile([P, 512], F32, name=f"xi{q}", align_bytes=64) for q in range(4)]
+
+        nc.vector.memset(ts[:].rearrange("p a t -> p (a t)").bitcast(I32), 0)
+        nc.vector.memset(w2s[:].rearrange("p a e -> p (a e)").bitcast(I32), 0)
+        nc.vector.memset(w4s[:].bitcast(I32), 0)
+
+        def load_table(a, lo, hi):
+            nc.sync.dma_start(out=tw[a][:, lo:hi].bitcast(I32),
+                              in_=tab_words[a].rearrange("p t i -> p (t i)").bitcast(I32)[:, lo:hi])
+
+        def load_weights(lo, hi):
+            for wi, w in enumerate((w1, w3)):
+                for a in range(PASSES):
+                    nc.sync.dma_start(out=raw[wi, lo, a][:],
+                                      in_=w[512 * a : 512 * (a + 1), lo * P : hi * P].rearrange("(p i) c -> p i c", i=4))
+
+        def load_page(dst, src, s):
+            nc.sync.dma_start(out=dst[s][:], in_=src[s * P : (s + 1) * P, :])
+
+        for lst, src in ((l1, offs), (l2, offs2), (l3, offs3), (l4, offs4)):
+            nc.sync.dma_start(lst[:], src)
+        nc.sync.dma_start(out=w2w[:].bitcast(I32), in_=w2_words.rearrange("a p e -> p a e").bitcast(I32))
+        for piece in range(3):
+            load_table(0, 512 * piece, 512 * (piece + 1))
+        for q in range(4):
+            nc.sync.dma_start(out=ts[32 * q : 32 * q + 4, :, :].bitcast(I32),
+                              in_=tab_scales[:, 4 * q : 4 * q + 4, :].rearrange("a r t -> r a t").bitcast(I32))
+        load_table(0, 512 * 3, T)
+        load_table(1, 0, T)
+        for q in range(4):
+            nc.sync.dma_start(out=w2s[32 * q : 32 * q + 4, :, :].bitcast(I32),
+                              in_=w2_scales[:, 4 * q : 4 * q + 4, :].rearrange("a r e -> r a e").bitcast(I32))
+        load_weights(0, 1)
+        nc.sync.dma_start(out=wgs_t[:, 0:QUARTER], in_=wgs[:, 0:QUARTER])
+        load_page(pg0, page0, 0)
+        nc.sync.dma_start(out=wgs_t[:, QUARTER:S], in_=wgs[:, QUARTER:S])
+        load_weights(1, 2)
+        with nc.allow_non_contiguous_dma(reason="one value a partition"):
+            nc.sync.dma_start(out=gain_t[:], in_=gain.rearrange("(s p) -> p s", p=P))
+            nc.sync.dma_start(out=res_t[:], in_=res.rearrange("(s p) -> p s", p=P))
+        load_weights(2, 4)
+        for s in range(1, SLICES):
+            load_page(pg0, page0, s)
+        nc.sync.dma_start(out=w4w[:].bitcast(I32), in_=w4_words[0].rearrange("p e i -> p (e i)").bitcast(I32))
+        for q in range(4):
+            nc.sync.dma_start(out=w4s[32 * q : 32 * q + 4, :].bitcast(I32),
+                              in_=w4_scales[0, 4 * q : 4 * q + 4, :].bitcast(I32))
+        nc.sync.dma_start(out=wgo_t[:], in_=wgo)
+        for s in range(SLICES):
+            load_page(pg1, page1, s)
+
+        for a in range(PASSES):
+            nc.vector.tensor_copy(vs[a][:], ts[:, a, :].indirect(l1[:]))
+        for a in range(PASSES):
+            nc.vector.tensor_copy(vw[a][:], tw[a][:].indirect(l1[:]))
+
+        make_identity(nc, id16[:])
+        make_identity(nc, id32[:])
+
+        def quantise_weight(wi, s):
+            lo = min(s, 2)
+            cols = slice((s - lo) * P, (s - lo + 1) * P)
+            dst = grp[wi, s][:].bitcast(BF16)
+            for a in range(PASSES):
+                view = dst[:, 512 * a : 512 * (a + 1)].rearrange("p (c i) -> p c i", i=4)
+                src = raw[wi, lo, a][:, :, cols].rearrange("p i c -> p c i")
+                nc.scalar.activation(out=view, in_=src, func=ACT.Copy, scale=-1.0 if wi == 0 else 1.0)
+            nc.vector.quantize_mx(out=wq[wi, s][:].bitcast(FP8X4), scales=wsc[wi, s][:], in_=dst)
+
+        quantise_weight(0, 0)
+        quantise_weight(1, 0)
+
+        def first_stage(s, lo, hi, d_sb, t_sb):
+            n = hi - lo
+            d_ps = psum.tile([P, 512], F32, name="d_ps", tag="d")
+            c_ps = psum.tile([P, 512], F32, name="c_ps", tag="c")
+            for a in range(PASSES):
+                wc = slice(a * P, (a + 1) * P)
+                rhs = vw[a][:, lo:hi].bitcast(FP8X4)
+                rsc = vs[a][:, lo:hi]
+                nc.tensor.matmul_mx(out=d_ps[:, 0:n], lhsT=wq[0, s][:, wc].bitcast(FP8X4), lhsT_scale=wsc[0, s][:, wc],
+                                    rhs=rhs, rhs_scale=rsc, start=(a == 0), stop=False)
+                nc.tensor.matmul_mx(out=d_ps[:, 0:n], lhsT=w2w[:, a, 2 * s * P : 2 * (s + 1) * P].bitcast(FP4X4),
+                                    lhsT_scale=w2s[:, a, s * P : (s + 1) * P],
+                                    rhs=rhs, rhs_scale=rsc, start=False, stop=(a == PASSES - 1))
+                nc.tensor.matmul_mx(out=c_ps[:, 0:n], lhsT=wq[1, s][:, wc].bitcast(FP8X4), lhsT_scale=wsc[1, s][:, wc],
+                                    rhs=rhs, rhs_scale=rsc, start=(a == 0), stop=(a == PASSES - 1))
+            nc.scalar.activation(out=d_sb, in_=d_ps[:, 0:n], func=ACT.Abs)
+            nc.vector.tensor_tensor(t_sb, c_ps[:, 0:n], wgs_t[:, lo:hi], ALU.mult)
+            nc.vector.tensor_tensor(pg0[s][:].indirect(entries(l2, lo, hi)), d_sb, t_sb, ALU.mult)
+
+        picked = {}
+        t1 = {}
+
+        def pick(s, lo, hi, g):
+            picked[s, lo] = g
+            nc.vector.tensor_copy(g, pg0[s][:].indirect(entries(l3, lo, hi)))
+
+        def turn(s, lo, hi, xb):
+            nc.scalar.activation(out=xb, in_=picked[s, lo], func=ACT.Copy, scale=gain_t[:, s : s + 1])
+            for q in range(lo // QUARTER, hi // QUARTER):
+                if q not in t1:
+                    t1[q] = psum.tile([P, 2, H], BF16, name="t1", tag="t1")
+                for b in range(2):
+                    c0 = q * QUARTER - lo + b * P
+                    nc.tensor.transpose(t1[q][:, b, s * P : (s + 1) * P], xb[:, c0 : c0 + P], id16[:])
+
+        def quantise_x(q):
+            words = t1[q][:].rearrange("j b r -> j (b r)").bitcast(F32)
+            nc.scalar.copy(out=xt[q][:].rearrange("j (b u p) -> j b u p", b=2, u=2),
+                           in_=words.rearrange("j (b p u) -> j b u p", b=2, u=2))
+            t2 = psum.tile([P, 2, 2, P], F32, name="t2", tag="t2")
+            for b in range(2):
+                for u in range(2):
+                    c0 = (2 * b + u) * P
+                    nc.tensor.transpose(t2[:, b, u, :], xt[q][:, c0 : c0 + P], id32[:])
+            nc.scalar.copy(out=xi[q][:].rearrange("p (b j u) -> p b j u", b=2, u=2),
+                           in_=t2[:].rearrange("p b u j -> p b j u"))
+            cols = slice(q * QUARTER, (q + 1) * QUARTER)
+            nc.vector.quantize_mx(out=xq[:, cols].bitcast(FP8X4), scales=xs[:, cols], in_=xi[q][:].bitcast(BF16))
+
+        def early_pick(s, lo):
+            g = keep.tile([P, QUARTER], F32, name=f"g{s}_{lo}")
+            pick(s, lo, lo + QUARTER, g[:])
+
+        def early_turn(s, lo):
+            if s < 2:
+                xb = raw[1, 2, 1][:, lo // QUARTER, s * P : (s + 1) * P].bitcast(BF16)
+            else:
+                xb_t = ring.tile([P, QUARTER], BF16, name="xb_t")
+                xb = xb_t[:]
+            turn(s, lo, lo + QUARTER, xb)
+
+        nc.vector.tensor_tensor(rg_t[:], res_t[:], gain_t[:], ALU.mult)
+
+        for s in range(SLICES):
+            width = QUARTER if s == 0 else 512
+            units = [(lo, lo + width) for lo in range(0, S, width)]
+            for i, (lo, hi) in enumerate(units):
+                wi = i - (len(units) - 2)
+                if s == SLICES - 1 and wi == 1:
+                    d_sb = late[:, 256:768]
+                    t_sb = late[:, 1024:1536]
+                else:
+                    d_t = ring.tile([P, 512], F32, name="d_t")
+                    d_sb = d_t[:, 0:width]
+                    if wi >= 0 and s < SLICES - 1:
+                        quantise_weight(wi, s + 1)
+                        t_sb = grp[wi, s + 1][:, 0:width]
+                    else:
+                        t_sb = grp[i % 2, 0][:, 0:width]
+                first_stage(s, lo, hi, d_sb, t_sb)
+            if s > 0:
+                early_turn(s - 1, 0)
+                early_turn(s - 1, QUARTER)
+            early_pick(s, 0)
+            early_pick(s, QUARTER)
+        early_turn(SLICES - 1, 0)
+        early_turn(SLICES - 1, QUARTER)
+
+        for s in range(SLICES - 1):
+            pick(s, 512, 1024, late[:, s * 512 : (s + 1) * 512])
+        quantise_x(0)
+        pick(SLICES - 1, 512, 1024, xi[0][:])
+
+        def second_stage(s, lo, hi, z):
+            n = hi - lo
+            e_ps = psum.tile([P, 512], F32, name="e_ps", tag="d" if s % 2 == 0 else "c")
+            nc.tensor.matmul_mx(out=e_ps[:, 0:n], lhsT=w4w[:, s * P : (s + 1) * P].bitcast(FP8X4),
+                                lhsT_scale=w4s[:, s * P : (s + 1) * P], rhs=xq[:, lo:hi].bitcast(FP8X4),
+                                rhs_scale=xs[:, lo:hi], start=True, stop=True)
+            nc.vector.scalar_tensor_tensor(out=z, in0=picked[s, lo], scalar=rg_t[:, s : s + 1],
+                                           in1=e_ps[:, 0:n], op0=ALU.mult, op1=ALU.add)
+            y = ring.tile([P, 512], F32, name="y", bufs=3)
+            nc.scalar.activation(out=y[:, 0:n], in_=z, func=ACT.Sigmoid)
+            nc.vector.tensor_tensor(pg1[s][:].indirect(entries(l4, lo, hi)), y[:, 0:n], wgo_t[:, lo:hi], ALU.mult)
+
+        def half(tile, h):
+            return tile[:, h * QUARTER : (h + 1) * QUARTER]
+
+        def ring_z(n):
+            z_t = ring.tile([P, 512], F32, name="z_t")
+            return z_t[:, 0:n]
+
+        for s in (0, 1):
+            second_stage(s, 0, QUARTER, half(xt[1], s))
+        quantise_x(1)
+        for s in (2, 3):
+            second_stage(s, 0, QUARTER, half(xi[1], s - 2))
+        for s in range(SLICES):
+            turn(s, 512, 1024, half(xt[1] if s < 2 else xi[1], s % 2).bitcast(BF16))
+        for s in (0, 1):
+            second_stage(s, QUARTER, 512, ring_z(QUARTER))
+        quantise_x(2)
+        quantise_x(3)
+        for s in (2, 3):
+            second_stage(s, QUARTER, 512, half(xi[3], s - 2))
+        for s in range(SLICES):
+            second_stage(s, 512, 1024, ring_z(512))
+            nc.sync.dma_start(out=out[s * P : (s + 1) * P, :], in_=pg1[s][:])

@@ -40,7 +40,7 @@ def tile_list_slab_vein_page_kernel(tc, tab_words, tab_scales, offs, w1, w2_word
         l3 = keep.tile([P, NP // 16], U16, name="l3")
         l4 = keep.tile([P, NP // 16], U16, name="l4")
         tw = [keep.tile([P, T], U32, name=f"tw{a}", align_bytes=64) for a in range(PASSES)]
-        ts = keep.tile([P, PASSES, T], U8, name="ts", align_bytes=64)
+        ts = keep.tile([P, T], U8, name="ts", align_bytes=64)
         vw = [keep.tile([P, S], U32, name=f"vw{a}", align_bytes=64) for a in range(PASSES)]
         vs = [keep.tile([P, S], U8, name=f"vs{a}", align_bytes=64) for a in range(PASSES)]
         w2w = keep.tile([P, PASSES, 2 * H], U8, name="w2w", align_bytes=64)
@@ -65,9 +65,10 @@ def tile_list_slab_vein_page_kernel(tc, tab_words, tab_scales, offs, w1, w2_word
         grp = {}
         wq = {}
         wsc = {}
+        both = [keep.tile([P, S + (QUARTER if s >= 2 else 0)], F32, name=f"both{s}", align_bytes=64) for s in range(SLICES)]
         for wi in range(2):
             for s in range(SLICES):
-                grp[wi, s] = keep.tile([P, 512], F32, name=f"grp{wi}_{s}", align_bytes=64)
+                grp[wi, s] = both[s][:, 512 * wi : 512 * (wi + 1)]
                 wq[wi, s] = keep.tile([P, PASSES * P], U32, name=f"wq{wi}_{s}", align_bytes=64)
                 wsc[wi, s] = keep.tile([P, PASSES * P], U8, name=f"wsc{wi}_{s}", align_bytes=64)
         late = keep.tile([P, 3 * 512], F32, name="late")
@@ -77,7 +78,8 @@ def tile_list_slab_vein_page_kernel(tc, tab_words, tab_scales, offs, w1, w2_word
         xt.append(xt[0])
         xi = [keep.tile([P, 512], F32, name=f"xi{q}", align_bytes=64) for q in range(4)]
 
-        nc.vector.memset(ts[:].rearrange("p a t -> p (a t)").bitcast(I32), 0)
+        nc.vector.memset(ts[:].bitcast(I32), 0)
+        nc.vector.memset(vs[1][:].bitcast(I32), 0)
         nc.vector.memset(w2s[:].rearrange("p a e -> p (a e)").bitcast(I32), 0)
         nc.vector.memset(w4s[:].bitcast(I32), 0)
 
@@ -99,25 +101,25 @@ def tile_list_slab_vein_page_kernel(tc, tab_words, tab_scales, offs, w1, w2_word
         nc.sync.dma_start(out=w2w[:].bitcast(I32), in_=w2_words.rearrange("a p e -> p a e").bitcast(I32))
         for piece in range(3):
             load_table(0, 512 * piece, 512 * (piece + 1))
-        for q in range(4):
-            nc.sync.dma_start(out=ts[32 * q : 32 * q + 4, :, :].bitcast(I32),
-                              in_=tab_scales[:, 4 * q : 4 * q + 4, :].rearrange("a r t -> r a t").bitcast(I32))
+        for q in (0, 2, 1, 3):
+            nc.sync.dma_start(out=ts[32 * q : 32 * q + 8, :].bitcast(I32),
+                              in_=tab_scales[:, 4 * q : 4 * q + 4, :].bitcast(I32))
         load_table(0, 512 * 3, T)
         load_table(1, 0, T)
         for q in range(4):
-            nc.sync.dma_start(out=w2s[32 * q : 32 * q + 4, :, :].bitcast(I32),
-                              in_=w2_scales[:, 4 * q : 4 * q + 4, :].rearrange("a r e -> r a e").bitcast(I32))
+            nc.gpsimd.dma_start(out=w2s[32 * q : 32 * q + 4, :, :].bitcast(I32),
+                                in_=w2_scales[:, 4 * q : 4 * q + 4, :].rearrange("a r e -> r a e").bitcast(I32))
         load_weights(0, 1)
         nc.sync.dma_start(out=wgs_t[:, 0:QUARTER], in_=wgs[:, 0:QUARTER])
         load_page(pg0, page0, 0)
         nc.sync.dma_start(out=wgs_t[:, QUARTER:S], in_=wgs[:, QUARTER:S])
         load_weights(1, 2)
-        with nc.allow_non_contiguous_dma(reason="one value a partition"):
-            nc.sync.dma_start(out=gain_t[:], in_=gain.rearrange("(s p) -> p s", p=P))
-            nc.sync.dma_start(out=res_t[:], in_=res.rearrange("(s p) -> p s", p=P))
         load_weights(2, 4)
         for s in range(1, SLICES):
             load_page(pg0, page0, s)
+        with nc.allow_non_contiguous_dma(reason="one value a partition"):
+            nc.sync.dma_start(out=gain_t[:], in_=gain.rearrange("(s p) -> p s", p=P))
+            nc.sync.dma_start(out=res_t[:], in_=res.rearrange("(s p) -> p s", p=P))
         nc.sync.dma_start(out=w4w[:].bitcast(I32), in_=w4_words[0].rearrange("p e i -> p (e i)").bitcast(I32))
         for q in range(4):
             nc.sync.dma_start(out=w4s[32 * q : 32 * q + 4, :].bitcast(I32),
@@ -126,8 +128,8 @@ def tile_list_slab_vein_page_kernel(tc, tab_words, tab_scales, offs, w1, w2_word
         for s in range(SLICES):
             load_page(pg1, page1, s)
 
-        for a in range(PASSES):
-            nc.vector.tensor_copy(vs[a][:], ts[:, a, :].indirect(l1[:]))
+        nc.vector.tensor_copy(vs[0][:], ts[:].indirect(l1[:]))
+        nc.scalar.dma_start(out=vs[1][0:112, :].bitcast(I32), in_=vs[0][4:116, :].bitcast(I32))
         for a in range(PASSES):
             nc.vector.tensor_copy(vw[a][:], tw[a][:].indirect(l1[:]))
 
@@ -137,7 +139,7 @@ def tile_list_slab_vein_page_kernel(tc, tab_words, tab_scales, offs, w1, w2_word
         def quantise_weight(wi, s):
             lo = min(s, 2)
             cols = slice((s - lo) * P, (s - lo + 1) * P)
-            dst = grp[wi, s][:].bitcast(BF16)
+            dst = grp[wi, s].bitcast(BF16)
             for a in range(PASSES):
                 view = dst[:, 512 * a : 512 * (a + 1)].rearrange("p (c i) -> p c i", i=4)
                 src = raw[wi, lo, a][:, :, cols].rearrange("p i c -> p c i")
@@ -145,26 +147,31 @@ def tile_list_slab_vein_page_kernel(tc, tab_words, tab_scales, offs, w1, w2_word
             nc.vector.quantize_mx(out=wq[wi, s][:].bitcast(FP8X4), scales=wsc[wi, s][:], in_=dst)
 
         quantise_weight(0, 0)
-        quantise_weight(1, 0)
+        for a in range(PASSES):
+            dst = grp[1, 0].bitcast(BF16)[:, 512 * a : 512 * (a + 1)]
+            nc.vector.tensor_copy(dst.rearrange("p (c i) -> p c i", i=4), raw[1, 0, a][:].rearrange("p i c -> p c i"))
+            wc = slice(a * P, (a + 1) * P)
+            nc.vector.quantize_mx(out=wq[1, 0][:, wc].bitcast(FP8X4), scales=wsc[1, 0][:, wc], in_=dst)
 
         def first_stage(s, lo, hi, d_sb, t_sb):
             n = hi - lo
-            d_ps = psum.tile([P, 512], F32, name="d_ps", tag="d")
-            c_ps = psum.tile([P, 512], F32, name="c_ps", tag="c")
+            d_ps = psum.tile([P, 512], F32, name="d_ps", tag="d", bufs=3)
+            c_ps = psum.tile([P, 512], F32, name="c_ps", tag="c", bufs=3)
             for a in range(PASSES):
                 wc = slice(a * P, (a + 1) * P)
                 rhs = vw[a][:, lo:hi].bitcast(FP8X4)
-                rsc = vs[a][:, lo:hi]
                 nc.tensor.matmul_mx(out=d_ps[:, 0:n], lhsT=wq[0, s][:, wc].bitcast(FP8X4), lhsT_scale=wsc[0, s][:, wc],
-                                    rhs=rhs, rhs_scale=rsc, start=(a == 0), stop=False)
+                                    rhs=rhs, rhs_scale=vs[0][4 * a : P, lo:hi], start=(a == 0), stop=False)
                 nc.tensor.matmul_mx(out=d_ps[:, 0:n], lhsT=w2w[:, a, 2 * s * P : 2 * (s + 1) * P].bitcast(FP4X4),
                                     lhsT_scale=w2s[:, a, s * P : (s + 1) * P],
-                                    rhs=rhs, rhs_scale=rsc, start=False, stop=(a == PASSES - 1))
+                                    rhs=rhs, rhs_scale=vs[a][:, lo:hi], start=False, stop=(a == PASSES - 1))
+            for a in range(PASSES):
+                wc = slice(a * P, (a + 1) * P)
                 nc.tensor.matmul_mx(out=c_ps[:, 0:n], lhsT=wq[1, s][:, wc].bitcast(FP8X4), lhsT_scale=wsc[1, s][:, wc],
-                                    rhs=rhs, rhs_scale=rsc, start=(a == 0), stop=(a == PASSES - 1))
+                                    rhs=vw[a][:, lo:hi].bitcast(FP8X4), rhs_scale=vs[0][4 * a : P, lo:hi],
+                                    start=(a == 0), stop=(a == PASSES - 1))
             nc.scalar.activation(out=d_sb, in_=d_ps[:, 0:n], func=ACT.Abs)
             nc.vector.tensor_tensor(t_sb, c_ps[:, 0:n], wgs_t[:, lo:hi], ALU.mult)
-            nc.vector.tensor_tensor(pg0[s][:].indirect(entries(l2, lo, hi)), d_sb, t_sb, ALU.mult)
 
         picked = {}
         t1 = {}
@@ -186,7 +193,7 @@ def tile_list_slab_vein_page_kernel(tc, tab_words, tab_scales, offs, w1, w2_word
             words = t1[q][:].rearrange("j b r -> j (b r)").bitcast(F32)
             nc.scalar.copy(out=xt[q][:].rearrange("j (b u p) -> j b u p", b=2, u=2),
                            in_=words.rearrange("j (b p u) -> j b u p", b=2, u=2))
-            t2 = psum.tile([P, 2, 2, P], F32, name="t2", tag="t2")
+            t2 = psum.tile([P, 2, 2, P], F32, name="t2", tag="c", bufs=3)
             for b in range(2):
                 for u in range(2):
                     c0 = (2 * b + u) * P
@@ -196,9 +203,15 @@ def tile_list_slab_vein_page_kernel(tc, tab_words, tab_scales, offs, w1, w2_word
             cols = slice(q * QUARTER, (q + 1) * QUARTER)
             nc.vector.quantize_mx(out=xq[:, cols].bitcast(FP8X4), scales=xs[:, cols], in_=xi[q][:].bitcast(BF16))
 
-        def early_pick(s, lo):
-            g = keep.tile([P, QUARTER], F32, name=f"g{s}_{lo}")
-            pick(s, lo, lo + QUARTER, g[:])
+        def early_pick(s):
+            g = keep.tile([P, 512], F32, name=f"g{s}")
+            if s < SLICES - 1:
+                pick(s, 0, 512, g[:])
+            else:
+                pick(s, 0, QUARTER, g[:, 0:QUARTER])
+                pick(s, QUARTER, 512, g[:, QUARTER:512])
+            picked[s, 0] = g[:, 0:QUARTER]
+            picked[s, QUARTER] = g[:, QUARTER:512]
 
         def early_turn(s, lo):
             if s < 2:
@@ -210,28 +223,37 @@ def tile_list_slab_vein_page_kernel(tc, tab_words, tab_scales, offs, w1, w2_word
 
         nc.vector.tensor_tensor(rg_t[:], res_t[:], gain_t[:], ALU.mult)
 
-        for s in range(SLICES):
-            width = QUARTER if s == 0 else 512
-            units = [(lo, lo + width) for lo in range(0, S, width)]
-            for i, (lo, hi) in enumerate(units):
-                wi = i - (len(units) - 2)
-                if s == SLICES - 1 and wi == 1:
-                    d_sb = late[:, 256:768]
-                    t_sb = late[:, 1024:1536]
-                else:
-                    d_t = ring.tile([P, 512], F32, name="d_t")
-                    d_sb = d_t[:, 0:width]
-                    if wi >= 0 and s < SLICES - 1:
-                        quantise_weight(wi, s + 1)
-                        t_sb = grp[wi, s + 1][:, 0:width]
-                    else:
-                        t_sb = grp[i % 2, 0][:, 0:width]
-                first_stage(s, lo, hi, d_sb, t_sb)
-            if s > 0:
-                early_turn(s - 1, 0)
-                early_turn(s - 1, QUARTER)
-            early_pick(s, 0)
-            early_pick(s, QUARTER)
+        def put(s, lo, hi, d_sb, t_sb):
+            nc.vector.tensor_tensor(pg0[s][:].indirect(entries(l2, lo, hi)), d_sb, t_sb, ALU.mult)
+
+        for i in range(4):
+            d_t = ring.tile([P, S], F32, name="d_t")
+            if i >= 2:
+                quantise_weight(i - 2, 1)
+            t_sb = grp[i % 2, i // 2][:, 0:QUARTER]
+            first_stage(0, i * QUARTER, (i + 1) * QUARTER, d_t[:, 0:QUARTER], t_sb)
+            put(0, i * QUARTER, (i + 1) * QUARTER, d_t[:, 0:QUARTER], t_sb)
+        early_pick(0)
+        for s in range(1, SLICES):
+            if s < SLICES - 1:
+                d_t = ring.tile([P, S], F32, name="d_t")
+                d_all = d_t[:]
+                t_all = both[s + 1][:, QUARTER : QUARTER + S]
+                quantise_weight(0, s + 1)
+                quantise_weight(1, s + 1)
+            else:
+                d_all = late[:, 256 : 256 + S]
+                t_all = both[0][:, 0:S]
+            for h in range(2):
+                cols = slice(512 * h, 512 * (h + 1))
+                first_stage(s, 512 * h, 512 * (h + 1), d_all[:, cols], t_all[:, cols])
+                if s == 1:
+                    put(s, 512 * h, 512 * (h + 1), d_all[:, cols], t_all[:, cols])
+            if s > 1:
+                put(s, 0, S, d_all, t_all)
+            early_turn(s - 1, 0)
+            early_turn(s - 1, QUARTER)
+            early_pick(s)
         early_turn(SLICES - 1, 0)
         early_turn(SLICES - 1, QUARTER)
 
@@ -242,7 +264,7 @@ def tile_list_slab_vein_page_kernel(tc, tab_words, tab_scales, offs, w1, w2_word
 
         def second_stage(s, lo, hi, z):
             n = hi - lo
-            e_ps = psum.tile([P, 512], F32, name="e_ps", tag="d" if s % 2 == 0 else "c")
+            e_ps = psum.tile([P, 512], F32, name="e_ps", tag="d" if s % 2 == 0 else "c", bufs=3)
             nc.tensor.matmul_mx(out=e_ps[:, 0:n], lhsT=w4w[:, s * P : (s + 1) * P].bitcast(FP8X4),
                                 lhsT_scale=w4s[:, s * P : (s + 1) * P], rhs=xq[:, lo:hi].bitcast(FP8X4),
                                 rhs_scale=xs[:, lo:hi], start=True, stop=True)

@@ -65,7 +65,7 @@ def tile_list_slab_vein_page_kernel(tc, tab_words, tab_scales, offs, w1, w2_word
         grp = {}
         wq = {}
         wsc = {}
-        both = [keep.tile([P, S + (QUARTER if s >= 2 else 0)], F32, name=f"both{s}", align_bytes=64) for s in range(SLICES)]
+        both = [keep.tile([P, S], F32, name=f"both{s}", align_bytes=64) for s in range(SLICES)]
         for wi in range(2):
             for s in range(SLICES):
                 grp[wi, s] = both[s][:, 512 * wi : 512 * (wi + 1)]
@@ -153,7 +153,7 @@ def tile_list_slab_vein_page_kernel(tc, tab_words, tab_scales, offs, w1, w2_word
             wc = slice(a * P, (a + 1) * P)
             nc.vector.quantize_mx(out=wq[1, 0][:, wc].bitcast(FP8X4), scales=wsc[1, 0][:, wc], in_=dst)
 
-        def first_stage(s, lo, hi, d_sb, t_sb):
+        def first_stage(s, lo, hi, d_sb, c_sb, v_sb):
             n = hi - lo
             d_ps = psum.tile([P, 512], F32, name="d_ps", tag="d", bufs=3)
             c_ps = psum.tile([P, 512], F32, name="c_ps", tag="c", bufs=3)
@@ -171,17 +171,24 @@ def tile_list_slab_vein_page_kernel(tc, tab_words, tab_scales, offs, w1, w2_word
                                     rhs=vw[a][:, lo:hi].bitcast(FP8X4), rhs_scale=vs[0][4 * a : P, lo:hi],
                                     start=(a == 0), stop=(a == PASSES - 1))
             nc.scalar.activation(out=d_sb, in_=d_ps[:, 0:n], func=ACT.Abs)
-            nc.vector.tensor_tensor(t_sb, c_ps[:, 0:n], wgs_t[:, lo:hi], ALU.mult)
+            if v_sb is None:
+                nc.vector.tensor_tensor(c_sb, c_ps[:, 0:n], wgs_t[:, lo:hi], ALU.mult)
+                nc.vector.tensor_tensor(pg0[s][:].indirect(entries(l2, lo, hi)), d_sb, c_sb, ALU.mult)
+            else:
+                nc.scalar.copy(out=c_sb, in_=c_ps[:, 0:n])
+                nc.gpsimd.tensor_tensor(d_sb, d_sb, c_sb, ALU.mult)
+                nc.gpsimd.tensor_tensor(v_sb, d_sb, wgs_t[:, lo:hi], ALU.mult)
 
         picked = {}
+        whole = {}
         t1 = {}
 
         def pick(s, lo, hi, g):
             picked[s, lo] = g
             nc.vector.tensor_copy(g, pg0[s][:].indirect(entries(l3, lo, hi)))
 
-        def turn(s, lo, hi, xb):
-            nc.scalar.activation(out=xb, in_=picked[s, lo], func=ACT.Copy, scale=gain_t[:, s : s + 1])
+        def turn(s, lo, hi, g, xb):
+            nc.scalar.activation(out=xb, in_=g, func=ACT.Copy, scale=gain_t[:, s : s + 1])
             for q in range(lo // QUARTER, hi // QUARTER):
                 if q not in t1:
                     t1[q] = psum.tile([P, 2, H], BF16, name="t1", tag="t1")
@@ -210,52 +217,53 @@ def tile_list_slab_vein_page_kernel(tc, tab_words, tab_scales, offs, w1, w2_word
             else:
                 pick(s, 0, QUARTER, g[:, 0:QUARTER])
                 pick(s, QUARTER, 512, g[:, QUARTER:512])
+            whole[s] = g[:]
             picked[s, 0] = g[:, 0:QUARTER]
             picked[s, QUARTER] = g[:, QUARTER:512]
 
-        def early_turn(s, lo):
-            if s < 2:
-                xb = raw[1, 2, 1][:, lo // QUARTER, s * P : (s + 1) * P].bitcast(BF16)
-            else:
-                xb_t = ring.tile([P, QUARTER], BF16, name="xb_t")
-                xb = xb_t[:]
-            turn(s, lo, lo + QUARTER, xb)
 
         nc.vector.tensor_tensor(rg_t[:], res_t[:], gain_t[:], ALU.mult)
 
-        def put(s, lo, hi, d_sb, t_sb):
-            nc.vector.tensor_tensor(pg0[s][:].indirect(entries(l2, lo, hi)), d_sb, t_sb, ALU.mult)
+        def put(s, lo, hi, v_sb):
+            nc.vector.tensor_copy(pg0[s][:].indirect(entries(l2, lo, hi)), v_sb)
 
+        d_own = [keep.tile([P, S], F32, name=f"d_own{s}") for s in range(2)]
+        d_of = [d_own[0][:], d_own[1][:], both[1][:], late[:, 256 : 256 + S]]
         for i in range(4):
-            d_t = ring.tile([P, S], F32, name="d_t")
-            if i >= 2:
-                quantise_weight(i - 2, 1)
-            t_sb = grp[i % 2, i // 2][:, 0:QUARTER]
-            first_stage(0, i * QUARTER, (i + 1) * QUARTER, d_t[:, 0:QUARTER], t_sb)
-            put(0, i * QUARTER, (i + 1) * QUARTER, d_t[:, 0:QUARTER], t_sb)
+            d_sb = d_of[0][:, i * QUARTER : (i + 1) * QUARTER]
+            c_sb = grp[i % 2, 0][:, 0:QUARTER]
+            if i == 0:
+                first_stage(0, 0, QUARTER, d_sb, c_sb, None)
+                continue
+            v_sb = d_sb
+            if i == 2:
+                quantise_weight(0, 1)
+                quantise_weight(1, 1)
+                v_sb = both[1][:, 384:640]
+            first_stage(0, i * QUARTER, (i + 1) * QUARTER, d_sb, c_sb, v_sb)
+            put(0, i * QUARTER, (i + 1) * QUARTER, v_sb)
         early_pick(0)
         for s in range(1, SLICES):
+            d_all = d_of[s]
             if s < SLICES - 1:
-                d_t = ring.tile([P, S], F32, name="d_t")
-                d_all = d_t[:]
-                t_all = both[s + 1][:, QUARTER : QUARTER + S]
                 quantise_weight(0, s + 1)
                 quantise_weight(1, s + 1)
-            else:
-                d_all = late[:, 256 : 256 + S]
-                t_all = both[0][:, 0:S]
             for h in range(2):
                 cols = slice(512 * h, 512 * (h + 1))
-                first_stage(s, 512 * h, 512 * (h + 1), d_all[:, cols], t_all[:, cols])
+                first_stage(s, 512 * h, 512 * (h + 1), d_all[:, cols], grp[h, 0], d_all[:, cols])
                 if s == 1:
-                    put(s, 512 * h, 512 * (h + 1), d_all[:, cols], t_all[:, cols])
+                    put(s, 512 * h, 512 * (h + 1), d_all[:, cols])
             if s > 1:
-                put(s, 0, S, d_all, t_all)
-            early_turn(s - 1, 0)
-            early_turn(s - 1, QUARTER)
+                put(s, 0, S, d_all)
+            if s == 2:
+                turn(0, 0, 512, whole[0], grp[1, 0][:, 0:QUARTER].bitcast(BF16))
+            if s == 3:
+                for r in (1, 2):
+                    turn(r, 0, 512, whole[r], grp[1, 0][:, (r - 1) * QUARTER : r * QUARTER].bitcast(BF16))
             early_pick(s)
-        early_turn(SLICES - 1, 0)
-        early_turn(SLICES - 1, QUARTER)
+        for lo in (0, QUARTER):
+            xb_t = ring.tile([P, QUARTER], BF16, name="xb_t")
+            turn(SLICES - 1, lo, lo + QUARTER, picked[SLICES - 1, lo], xb_t[:])
 
         for s in range(SLICES - 1):
             pick(s, 512, 1024, late[:, s * 512 : (s + 1) * 512])
@@ -287,7 +295,7 @@ def tile_list_slab_vein_page_kernel(tc, tab_words, tab_scales, offs, w1, w2_word
         for s in (2, 3):
             second_stage(s, 0, QUARTER, half(xi[1], s - 2))
         for s in range(SLICES):
-            turn(s, 512, 1024, half(xt[1] if s < 2 else xi[1], s % 2).bitcast(BF16))
+            turn(s, 512, 1024, picked[s, 512], half(xt[1] if s < 2 else xi[1], s % 2).bitcast(BF16))
         for s in (0, 1):
             second_stage(s, QUARTER, 512, ring_z(QUARTER))
         quantise_x(2)

@@ -56,7 +56,7 @@ def tile_list_slab_vein_page_kernel(tc, tab_words, tab_scales, offs, w1, w2_word
         rg_t = keep.tile([P, SLICES], F32, name="rg_t")
         id16 = keep.tile([P, P], BF16, name="id16")
         id32 = keep.tile([P, P], F32, name="id32")
-        groups = [(0, 1), (1, 2), (2, 4)]
+        groups = [(s, s + 1) for s in range(SLICES)]
         raw = {}
         for wi in range(2):
             for lo, hi in groups:
@@ -71,6 +71,9 @@ def tile_list_slab_vein_page_kernel(tc, tab_words, tab_scales, offs, w1, w2_word
                 grp[wi, s] = both[s][:, 512 * wi : 512 * (wi + 1)]
                 wq[wi, s] = keep.tile([P, PASSES * P], U32, name=f"wq{wi}_{s}", align_bytes=64)
                 wsc[wi, s] = keep.tile([P, PASSES * P], U8, name=f"wsc{wi}_{s}", align_bytes=64)
+        early = [keep.tile([P, 512], F32, name=f"early{s}", align_bytes=64) for s in range(SLICES)]
+        grp[1, 1] = early[0][:]
+        grp[1, 3] = early[1][:]
         late = keep.tile([P, 3 * 512], F32, name="late")
         xq = keep.tile([P, NP], U32, name="xq", align_bytes=64)
         xs = keep.tile([P, NP], U8, name="xs", align_bytes=64)
@@ -114,8 +117,10 @@ def tile_list_slab_vein_page_kernel(tc, tab_words, tab_scales, offs, w1, w2_word
         load_page(pg0, page0, 0)
         nc.sync.dma_start(out=wgs_t[:, QUARTER:S], in_=wgs[:, QUARTER:S])
         load_weights(1, 2)
-        load_weights(2, 4)
-        for s in range(1, SLICES):
+        load_weights(2, 3)
+        load_page(pg0, page0, 1)
+        load_weights(3, 4)
+        for s in range(2, SLICES):
             load_page(pg0, page0, s)
         with nc.allow_non_contiguous_dma(reason="one value a partition"):
             nc.sync.dma_start(out=gain_t[:], in_=gain.rearrange("(s p) -> p s", p=P))
@@ -137,7 +142,7 @@ def tile_list_slab_vein_page_kernel(tc, tab_words, tab_scales, offs, w1, w2_word
         make_identity(nc, id32[:])
 
         def quantise_weight(wi, s):
-            lo = min(s, 2)
+            lo = s
             cols = slice((s - lo) * P, (s - lo + 1) * P)
             dst = grp[wi, s].bitcast(BF16)
             for a in range(PASSES):
@@ -174,6 +179,9 @@ def tile_list_slab_vein_page_kernel(tc, tab_words, tab_scales, offs, w1, w2_word
             if v_sb is None:
                 nc.vector.tensor_tensor(c_sb, c_ps[:, 0:n], wgs_t[:, lo:hi], ALU.mult)
                 nc.vector.tensor_tensor(pg0[s][:].indirect(entries(l2, lo, hi)), d_sb, c_sb, ALU.mult)
+            elif (s, lo) == (1, 0):
+                nc.vector.tensor_tensor(c_sb, c_ps[:, 0:n], wgs_t[:, lo:hi], ALU.mult)
+                nc.gpsimd.tensor_tensor(v_sb, d_sb, c_sb, ALU.mult)
             else:
                 nc.scalar.copy(out=c_sb, in_=c_ps[:, 0:n])
                 nc.gpsimd.tensor_tensor(d_sb, d_sb, c_sb, ALU.mult)
@@ -211,7 +219,7 @@ def tile_list_slab_vein_page_kernel(tc, tab_words, tab_scales, offs, w1, w2_word
             nc.vector.quantize_mx(out=xq[:, cols].bitcast(FP8X4), scales=xs[:, cols], in_=xi[q][:].bitcast(BF16))
 
         def early_pick(s):
-            g = keep.tile([P, 512], F32, name=f"g{s}")
+            g = early[s]
             if s < SLICES - 1:
                 pick(s, 0, 512, g[:])
             else:
@@ -236,25 +244,29 @@ def tile_list_slab_vein_page_kernel(tc, tab_words, tab_scales, offs, w1, w2_word
                 first_stage(0, 0, QUARTER, d_sb, c_sb, None)
                 continue
             v_sb = d_sb
-            if i == 2:
+            if i == 3:
                 quantise_weight(0, 1)
                 quantise_weight(1, 1)
-                v_sb = both[1][:, 384:640]
+                v_sb = grp[0, 1][:, 0:QUARTER]
             first_stage(0, i * QUARTER, (i + 1) * QUARTER, d_sb, c_sb, v_sb)
             put(0, i * QUARTER, (i + 1) * QUARTER, v_sb)
         early_pick(0)
         for s in range(1, SLICES):
             d_all = d_of[s]
-            if s < SLICES - 1:
-                quantise_weight(0, s + 1)
-                quantise_weight(1, s + 1)
-            for h in range(2):
-                cols = slice(512 * h, 512 * (h + 1))
-                first_stage(s, 512 * h, 512 * (h + 1), d_all[:, cols], grp[h, 0], d_all[:, cols])
-                if s == 1:
-                    put(s, 512 * h, 512 * (h + 1), d_all[:, cols])
-            if s > 1:
+            if s == 1:
+                quantise_weight(0, 2)
+                quantise_weight(1, 2)
+            cuts = (0, QUARTER, 512, S) if s == 1 else (0, 512, S)
+            for lo, hi in zip(cuts, cuts[1:]):
+                v_sb = grp[0, 3] if (s, lo) == (2, 0) else d_all[:, lo:hi]
+                first_stage(s, lo, hi, d_all[:, lo:hi], both[0][:, lo:hi], v_sb)
+                if s < SLICES - 1:
+                    put(s, lo, hi, v_sb)
+            if s == SLICES - 1:
                 put(s, 0, S, d_all)
+            if s == 1:
+                quantise_weight(0, 3)
+                quantise_weight(1, 3)
             if s == 2:
                 turn(0, 0, 512, whole[0], grp[1, 0][:, 0:QUARTER].bitcast(BF16))
             if s == 3:

from contextlib import ExitStack

import concourse.mybir as mybir
from concourse.masks import make_identity

K, H, T, S, T2, NP = 1024, 512, 4096, 1024, 2048, 1024
FLOPS = 2 * 3 * K * H * S + 2 * H * H * NP

F32 = mybir.dt.float32
BF16 = mybir.dt.bfloat16
I32 = mybir.dt.int32
U32 = mybir.dt.uint32
U16 = mybir.dt.uint16
U8 = mybir.dt.uint8
FP8X4 = mybir.dt.float8_e4m3fn_x4
FP4X4 = mybir.dt.float4_e2m1fn_x4
ACT = mybir.ActivationFunctionType
ALU = mybir.AluOpType

P = 128
PASSES = K // 512
SLICES = H // P
QUARTER = 256


def tile_list_slab_vein_page_kernel(tc, tab_words, tab_scales, offs, w1, w2_words, w2_scales, w3, page0,
                                             wgs, offs2, offs3, gain, w4_words, w4_scales, res, page1, wgo, offs4,
                                             out):
    nc = tc.nc
    with ExitStack() as ctx:
        keep = ctx.enter_context(tc.tile_pool(name="keep", bufs=1))
        ring = ctx.enter_context(tc.tile_pool(name="ring", bufs=2))
        psum = ctx.enter_context(tc.psum_pool(name="psum", bufs=2))

        def entries(lst, lo, hi):
            return lst[:, lo // 16 : hi // 16]

        l1 = keep.tile([P, S // 16], U16, name="l1")
        l2 = keep.tile([P, S // 16], U16, name="l2")
        l3 = keep.tile([P, NP // 16], U16, name="l3")
        l4 = keep.tile([P, NP // 16], U16, name="l4")
        tw = [keep.tile([P, T], U32, name=f"tw{a}", align_bytes=64) for a in range(PASSES)]
        ts = keep.tile([P, T], U8, name="ts", align_bytes=64)
        vw = [keep.tile([P, S], U32, name=f"vw{a}", align_bytes=64) for a in range(PASSES)]
        vs = [keep.tile([P, S], U8, name=f"vs{a}", align_bytes=64) for a in range(PASSES)]
        w2w = keep.tile([P, PASSES, 2 * H], U8, name="w2w", align_bytes=64)
        w2s = keep.tile([P, PASSES, H], U8, name="w2s", align_bytes=64)
        w4w = keep.tile([P, H], U32, name="w4w", align_bytes=64)
        w4s = keep.tile([P, H], U8, name="w4s", align_bytes=64)
        pg0 = [keep.tile([P, T2], F32, name=f"pg0_{s}") for s in range(SLICES)]
        pg1 = [keep.tile([P, T2], F32, name=f"pg1_{s}") for s in range(SLICES)]
        wgs_t = keep.tile([P, S], F32, name="wgs_t")
        wgo_t = keep.tile([P, NP], F32, name="wgo_t")
        gain_t = keep.tile([P, SLICES], F32, name="gain_t")
        res_t = keep.tile([P, SLICES], F32, name="res_t")
        rg_t = keep.tile([P, SLICES], F32, name="rg_t")
        id16 = keep.tile([P, P], BF16, name="id16")
        id32 = keep.tile([P, P], F32, name="id32")
        groups = [(s, s + 1) for s in range(SLICES)]
        raw = {}
        for wi in range(2):
            for lo, hi in groups:
                for a in range(PASSES):
                    raw[wi, lo, a] = keep.tile([P, 4, (hi - lo) * P], F32, name=f"raw{wi}_{lo}_{a}")
        grp = {}
        wq = {}
        wsc = {}
        both = [keep.tile([P, S], F32, name=f"both{s}", align_bytes=64) for s in range(SLICES)]
        for wi in range(2):
            for s in range(SLICES):
                grp[wi, s] = both[s][:, 512 * wi : 512 * (wi + 1)]
                wq[wi, s] = keep.tile([P, PASSES * P], U32, name=f"wq{wi}_{s}", align_bytes=64)
                wsc[wi, s] = keep.tile([P, PASSES * P], U8, name=f"wsc{wi}_{s}", align_bytes=64)
        early = [keep.tile([P, 512], F32, name=f"early{s}", align_bytes=64) for s in range(SLICES)]
        grp[1, 1] = early[0][:]
        grp[1, 3] = early[1][:]
        late = keep.tile([P, 3 * 512], F32, name="late")
        xq = keep.tile([P, NP], U32, name="xq", align_bytes=64)
        xs = keep.tile([P, NP], U8, name="xs", align_bytes=64)
        xt = [keep.tile([P, 512], F32, name=f"xt{q}", align_bytes=64) for q in range(3)]
        xt.append(xt[0])
        xi = [keep.tile([P, 512], F32, name=f"xi{q}", align_bytes=64) for q in range(4)]

        nc.vector.memset(ts[:].bitcast(I32), 0)
        nc.vector.memset(vs[1][:].bitcast(I32), 0)
        nc.vector.memset(w2s[:].rearrange("p a e -> p (a e)").bitcast(I32), 0)
        nc.vector.memset(w4s[:].bitcast(I32), 0)

        def load_table(a, lo, hi):
            nc.sync.dma_start(out=tw[a][:, lo:hi].bitcast(I32),
                              in_=tab_words[a].rearrange("p t i -> p (t i)").bitcast(I32)[:, lo:hi])

        def load_weights(lo, hi):
            for wi, w in enumerate((w1, w3)):
                for a in range(PASSES):
                    nc.sync.dma_start(out=raw[wi, lo, a][:],
                                      in_=w[512 * a : 512 * (a + 1), lo * P : hi * P].rearrange("(p i) c -> p i c", i=4))

        def load_page(dst, src, s):
            nc.sync.dma_start(out=dst[s][:], in_=src[s * P : (s + 1) * P, :])

        for lst, src in ((l1, offs), (l2, offs2), (l3, offs3), (l4, offs4)):
            nc.sync.dma_start(lst[:], src)
        nc.sync.dma_start(out=w2w[:].bitcast(I32), in_=w2_words.rearrange("a p e -> p a e").bitcast(I32))
        for piece in range(3):
            load_table(0, 512 * piece, 512 * (piece + 1))
        for q in (0, 2, 1, 3):
            nc.sync.dma_start(out=ts[32 * q : 32 * q + 8, :].bitcast(I32),
                              in_=tab_scales[:, 4 * q : 4 * q + 4, :].bitcast(I32))
        load_table(0, 512 * 3, T)
        load_table(1, 0, T)
        for q in range(4):
            nc.gpsimd.dma_start(out=w2s[32 * q : 32 * q + 4, :, :].bitcast(I32),
                                in_=w2_scales[:, 4 * q : 4 * q + 4, :].rearrange("a r e -> r a e").bitcast(I32))
        load_weights(0, 1)
        nc.sync.dma_start(out=wgs_t[:, 0:QUARTER], in_=wgs[:, 0:QUARTER])
        load_page(pg0, page0, 0)
        nc.sync.dma_start(out=wgs_t[:, QUARTER:S], in_=wgs[:, QUARTER:S])
        load_weights(1, 2)
        load_weights(2, 3)
        load_page(pg0, page0, 1)
        load_weights(3, 4)
        for s in range(2, SLICES):
            load_page(pg0, page0, s)
        with nc.allow_non_contiguous_dma(reason="one value a partition"):
            nc.sync.dma_start(out=gain_t[:], in_=gain.rearrange("(s p) -> p s", p=P))
            nc.sync.dma_start(out=res_t[:], in_=res.rearrange("(s p) -> p s", p=P))
        nc.sync.dma_start(out=w4w[:].bitcast(I32), in_=w4_words[0].rearrange("p e i -> p (e i)").bitcast(I32))
        for q in range(4):
            nc.sync.dma_start(out=w4s[32 * q : 32 * q + 4, :].bitcast(I32),
                              in_=w4_scales[0, 4 * q : 4 * q + 4, :].bitcast(I32))
        nc.sync.dma_start(out=wgo_t[:], in_=wgo)
        for s in range(SLICES):
            load_page(pg1, page1, s)

        nc.vector.tensor_copy(vs[0][:], ts[:].indirect(l1[:]))
        nc.scalar.dma_start(out=vs[1][0:112, :].bitcast(I32), in_=vs[0][4:116, :].bitcast(I32))
        for a in range(PASSES):
            nc.vector.tensor_copy(vw[a][:], tw[a][:].indirect(l1[:]))

        make_identity(nc, id16[:])
        make_identity(nc, id32[:])

        def quantise_weight(wi, s):
            lo = s
            cols = slice((s - lo) * P, (s - lo + 1) * P)
            dst = grp[wi, s].bitcast(BF16)
            for a in range(PASSES):
                view = dst[:, 512 * a : 512 * (a + 1)].rearrange("p (c i) -> p c i", i=4)
                src = raw[wi, lo, a][:, :, cols].rearrange("p i c -> p c i")
                nc.scalar.activation(out=view, in_=src, func=ACT.Copy, scale=-1.0 if wi == 0 else 1.0)
            nc.vector.quantize_mx(out=wq[wi, s][:].bitcast(FP8X4), scales=wsc[wi, s][:], in_=dst)

        quantise_weight(0, 0)
        for a in range(PASSES):
            dst = grp[1, 0].bitcast(BF16)[:, 512 * a : 512 * (a + 1)]
            nc.vector.tensor_copy(dst.rearrange("p (c i) -> p c i", i=4), raw[1, 0, a][:].rearrange("p i c -> p c i"))
            wc = slice(a * P, (a + 1) * P)
            nc.vector.quantize_mx(out=wq[1, 0][:, wc].bitcast(FP8X4), scales=wsc[1, 0][:, wc], in_=dst)

        def first_stage(s, lo, hi, d_sb, c_sb, v_sb):
            n = hi - lo
            d_ps = psum.tile([P, 512], F32, name="d_ps", tag="d", bufs=3)
            c_ps = psum.tile([P, 512], F32, name="c_ps", tag="c", bufs=3)
            for a in range(PASSES):
                wc = slice(a * P, (a + 1) * P)
                rhs = vw[a][:, lo:hi].bitcast(FP8X4)
                nc.tensor.matmul_mx(out=d_ps[:, 0:n], lhsT=wq[0, s][:, wc].bitcast(FP8X4), lhsT_scale=wsc[0, s][:, wc],
                                    rhs=rhs, rhs_scale=vs[0][4 * a : P, lo:hi], start=(a == 0), stop=False)
                nc.tensor.matmul_mx(out=d_ps[:, 0:n], lhsT=w2w[:, a, 2 * s * P : 2 * (s + 1) * P].bitcast(FP4X4),
                                    lhsT_scale=w2s[:, a, s * P : (s + 1) * P],
                                    rhs=rhs, rhs_scale=vs[a][:, lo:hi], start=False, stop=(a == PASSES - 1))
            for a in range(PASSES):
                wc = slice(a * P, (a + 1) * P)
                nc.tensor.matmul_mx(out=c_ps[:, 0:n], lhsT=wq[1, s][:, wc].bitcast(FP8X4), lhsT_scale=wsc[1, s][:, wc],
                                    rhs=vw[a][:, lo:hi].bitcast(FP8X4), rhs_scale=vs[0][4 * a : P, lo:hi],
                                    start=(a == 0), stop=(a == PASSES - 1))
            nc.scalar.activation(out=d_sb, in_=d_ps[:, 0:n], func=ACT.Abs)
            if v_sb is None:
                nc.vector.tensor_tensor(c_sb, c_ps[:, 0:n], wgs_t[:, lo:hi], ALU.mult)
                nc.vector.tensor_tensor(pg0[s][:].indirect(entries(l2, lo, hi)), d_sb, c_sb, ALU.mult)
            elif (s, lo) == (1, 0):
                nc.vector.tensor_tensor(c_sb, c_ps[:, 0:n], wgs_t[:, lo:hi], ALU.mult)
                nc.gpsimd.tensor_tensor(v_sb, d_sb, c_sb, ALU.mult)
            else:
                nc.scalar.copy(out=c_sb, in_=c_ps[:, 0:n])
                nc.gpsimd.tensor_tensor(d_sb, d_sb, c_sb, ALU.mult)
                nc.gpsimd.tensor_tensor(v_sb, d_sb, wgs_t[:, lo:hi], ALU.mult)

        picked = {}
        whole = {}
        t1 = {}

        def pick(s, lo, hi, g):
            picked[s, lo] = g
            nc.vector.tensor_copy(g, pg0[s][:].indirect(entries(l3, lo, hi)))

        def turn(s, lo, hi, g, xb):
            nc.scalar.activation(out=xb, in_=g, func=ACT.Copy, scale=gain_t[:, s : s + 1])
            for q in range(lo // QUARTER, hi // QUARTER):
                if q not in t1:
                    t1[q] = psum.tile([P, 2, H], BF16, name="t1", tag="t1")
                for b in range(2):
                    c0 = q * QUARTER - lo + b * P
                    nc.tensor.transpose(t1[q][:, b, s * P : (s + 1) * P], xb[:, c0 : c0 + P], id16[:])

        def quantise_x(q):
            words = t1[q][:].rearrange("j b r -> j (b r)").bitcast(F32)
            nc.scalar.copy(out=xt[q][:].rearrange("j (b u p) -> j b u p", b=2, u=2),
                           in_=words.rearrange("j (b p u) -> j b u p", b=2, u=2))
            t2 = psum.tile([P, 2, 2, P], F32, name="t2", tag="c", bufs=3)
            for b in range(2):
                for u in range(2):
                    c0 = (2 * b + u) * P
                    nc.tensor.transpose(t2[:, b, u, :], xt[q][:, c0 : c0 + P], id32[:])
            nc.scalar.copy(out=xi[q][:].rearrange("p (b j u) -> p b j u", b=2, u=2),
                           in_=t2[:].rearrange("p b u j -> p b j u"))
            cols = slice(q * QUARTER, (q + 1) * QUARTER)
            nc.vector.quantize_mx(out=xq[:, cols].bitcast(FP8X4), scales=xs[:, cols], in_=xi[q][:].bitcast(BF16))

        def early_pick(s):
            g = early[s]
            if s < SLICES - 1:
                pick(s, 0, 512, g[:])
            else:
                pick(s, 0, QUARTER, g[:, 0:QUARTER])
                pick(s, QUARTER, 512, g[:, QUARTER:512])
            whole[s] = g[:]
            picked[s, 0] = g[:, 0:QUARTER]
            picked[s, QUARTER] = g[:, QUARTER:512]


        nc.vector.tensor_tensor(rg_t[:], res_t[:], gain_t[:], ALU.mult)

        def put(s, lo, hi, v_sb):
            nc.vector.tensor_copy(pg0[s][:].indirect(entries(l2, lo, hi)), v_sb)

        d_own = [keep.tile([P, S], F32, name=f"d_own{s}") for s in range(2)]
        d_of = [d_own[0][:], d_own[1][:], both[1][:], late[:, 256 : 256 + S]]
        for i in range(4):
            d_sb = d_of[0][:, i * QUARTER : (i + 1) * QUARTER]
            c_sb = grp[i % 2, 0][:, 0:QUARTER]
            if i == 0:
                first_stage(0, 0, QUARTER, d_sb, c_sb, None)
                continue
            v_sb = d_sb
            if i == 3:
                quantise_weight(0, 1)
                quantise_weight(1, 1)
                v_sb = grp[0, 1][:, 0:QUARTER]
            first_stage(0, i * QUARTER, (i + 1) * QUARTER, d_sb, c_sb, v_sb)
            put(0, i * QUARTER, (i + 1) * QUARTER, v_sb)
        early_pick(0)
        for s in range(1, SLICES):
            d_all = d_of[s]
            if s == 1:
                quantise_weight(0, 2)
                quantise_weight(1, 2)
            cuts = (0, QUARTER, 512, S) if s == 1 else (0, 512, S)
            for lo, hi in zip(cuts, cuts[1:]):
                v_sb = grp[0, 3] if (s, lo) == (2, 0) else d_all[:, lo:hi]
                first_stage(s, lo, hi, d_all[:, lo:hi], both[0][:, lo:hi], v_sb)
                if s < SLICES - 1:
                    put(s, lo, hi, v_sb)
            if s == SLICES - 1:
                put(s, 0, S, d_all)
            if s == 1:
                quantise_weight(0, 3)
                quantise_weight(1, 3)
            if s == 2:
                turn(0, 0, 512, whole[0], grp[1, 0][:, 0:QUARTER].bitcast(BF16))
            if s == 3:
                for r in (1, 2):
                    turn(r, 0, 512, whole[r], grp[1, 0][:, (r - 1) * QUARTER : r * QUARTER].bitcast(BF16))
            early_pick(s)
        for lo in (0, QUARTER):
            xb_t = ring.tile([P, QUARTER], BF16, name="xb_t")
            turn(SLICES - 1, lo, lo + QUARTER, picked[SLICES - 1, lo], xb_t[:])

        for s in range(SLICES - 1):
            pick(s, 512, 1024, late[:, s * 512 : (s + 1) * 512])
        quantise_x(0)
        pick(SLICES - 1, 512, 1024, xi[0][:])

        def second_stage(s, lo, hi, z):
            n = hi - lo
            e_ps = psum.tile([P, 512], F32, name="e_ps", tag="d" if s % 2 == 0 else "c", bufs=3)
            nc.tensor.matmul_mx(out=e_ps[:, 0:n], lhsT=w4w[:, s * P : (s + 1) * P].bitcast(FP8X4),
                                lhsT_scale=w4s[:, s * P : (s + 1) * P], rhs=xq[:, lo:hi].bitcast(FP8X4),
                                rhs_scale=xs[:, lo:hi], start=True, stop=True)
            nc.vector.scalar_tensor_tensor(out=z, in0=picked[s, lo], scalar=rg_t[:, s : s + 1],
                                           in1=e_ps[:, 0:n], op0=ALU.mult, op1=ALU.add)
            y = ring.tile([P, 512], F32, name="y", bufs=3)
            nc.scalar.activation(out=y[:, 0:n], in_=z, func=ACT.Sigmoid)
            nc.vector.tensor_tensor(pg1[s][:].indirect(entries(l4, lo, hi)), y[:, 0:n], wgo_t[:, lo:hi], ALU.mult)

        def half(tile, h):
            return tile[:, h * QUARTER : (h + 1) * QUARTER]

        def ring_z(n):
            z_t = ring.tile([P, 512], F32, name="z_t")
            return z_t[:, 0:n]

        for s in (0, 1):
            second_stage(s, 0, QUARTER, half(xt[1], s))
        quantise_x(1)
        for s in (2, 3):
            second_stage(s, 0, QUARTER, half(xi[1], s - 2))
        for s in range(SLICES):
            turn(s, 512, 1024, picked[s, 512], half(xt[1] if s < 2 else xi[1], s % 2).bitcast(BF16))
        for s in (0, 1):
            second_stage(s, QUARTER, 512, ring_z(QUARTER))
        quantise_x(2)
        quantise_x(3)
        for s in (2, 3):
            second_stage(s, QUARTER, 512, half(xi[3], s - 2))
        for s in range(SLICES):
            second_stage(s, 512, 1024, ring_z(512))
            nc.sync.dma_start(out=out[s * P : (s + 1) * P, :], in_=pg1[s][:])
